import numpy as np, ml_dtypes
CORES = [56,64,184,192,312,320,440,448]
N = 8
NP, NBK, TK, CAP = 4, 2, 256, 5
DEST = [[4,4],[5,4],[7,6],[4,4]]
def setup_inputs(rng):
    return {"x": rng.standard_normal((N, 128, NBK * TK), dtype=np.float32).astype(ml_dtypes.bfloat16), "w": (rng.standard_normal((N, 128, 128), dtype=np.float32) / 8).astype(ml_dtypes.bfloat16)}
def setup_inputs_big(rng):
    d = setup_inputs(rng)
    for k in ("x", "w"): d[k] = (d[k].astype(np.float32) * 1024.0).astype(d[k].dtype)
    return d
def setup_inputs_small(rng):
    d = setup_inputs(rng)
    for k in ("x", "w"): d[k] = (d[k].astype(np.float32) * (1 / 1024.0)).astype(d[k].dtype)
    return d
def setup_inputs_apart(rng):
    d = setup_inputs(rng)
    f = (10.0 ** rng.permutation(np.linspace(-1.5, 1.5, N))).astype(np.float32).reshape(N, 1, 1)
    for k in ("x", "w"): d[k] = (d[k].astype(np.float32) * f).astype(d[k].dtype)
    return d
def reference(x, w):
    X, W = x.astype(np.float64), w.astype(np.float64)
    y = np.full((N, 128, CAP * TK), np.nan); n = [0] * N
    for p in range(NP):
        for c in range(NBK):
            q = DEST[p][c]
            y[q][:, TK * n[q]:TK * n[q] + TK] = W[q].T @ np.maximum(W[p].T @ X[p][:, TK * c:TK * c + TK], 0.0)
            n[q] += 1
    return {"y": y.astype(ml_dtypes.bfloat16 if x.dtype != np.float64 else np.float64)}

@@ -1,0 +1,160 @@
+from concourse.mybir import AluOpType
+
+TK, SLOTS, BAYS = 256, 5, 2
+
+SCRATCH = {
+    "xs": ("sbuf", [128, 2 * TK], "bfloat16"),
+    "ws": ("sbuf", [128, 128], "bfloat16"),
+    "zero": ("sbuf", [128, TK], "float32"),
+    "h0": ("sbuf", [128, TK], "bfloat16"),
+    "h1": ("sbuf", [128, TK], "bfloat16"),
+    "bay0": ("sbuf", [128, TK], "bfloat16"),
+    "bay1": ("sbuf", [128, TK], "bfloat16"),
+    "land": ("sbuf", [128, SLOTS * TK], "bfloat16"),
+    "res": ("sbuf", [128, SLOTS * TK], "bfloat16"),
+}
+for _i in range(SLOTS):
+    SCRATCH["ps%d" % _i] = ("psum", [128, 512], "float32")
+
+SEMAPHORES = ["wl", "xl0", "xl1", "zs", "sent", "in0", "in1"] + [
+    "%s%d" % (n, i) for n in ("at", "mm", "cp", "st") for i in range(SLOTS)]
+
+_MEMO = {}
+
+
+def _routes(cores, dest, topo):
+    if "routes" in _MEMO:
+        return _MEMO["routes"]
+    per_host = topo.CORES_PER_HOST
+    world = range(per_host * (1 + max(topo.host(c) for c in cores)))
+    senders = cores[:len(dest)]
+    mate_memo = {}
+
+    def place(c):
+        return (topo.host(c), topo.chip(c))
+
+    def mate_core(c):
+        if place(c) not in mate_memo:
+            mate_memo[place(c)] = [m for m in world if topo.mates(c, m)][0]
+        return mate_memo[place(c)]
+
+    def twin(c, h):
+        return c % per_host + h * per_host
+
+    def cable(c, at):
+        return ("cable", place(at), topo.die(c), topo.may_write(c, mate_core(c)))
+
+    def in_rack(a, b, d):
+        if place(a) == place(b):
+            return []
+        if topo.mates(a, b):
+            return [("mate", place(a), d)]
+        if topo.same_plane(a, b):
+            return [("out", place(a), d), ("in", place(b), d)]
+        return [("mate", place(a), d)] + in_rack(mate_core(a), b, d)
+
+    def ways(a, b):
+        d, ha, hb = topo.die(a), topo.host(a), topo.host(b)
+        if topo.rack(ha) == topo.rack(hb):
+            return [in_rack(a, b, d)]
+        first = [cable(a, a)] + in_rack(twin(a, hb), b, d)
+        if topo.chip(a) == topo.chip(b):
+            return [first]
+        return [first, in_rack(a, twin(b, ha), d) + [cable(a, twin(b, ha))]]
+
+    def length(w1, w2):
+        return sum(max(len([k for k in w if k[0] != "in"]) for w in ww) + len(ww) - 1 for ww in (w1, w2))
+
+    def relays(src, dst, bays):
+        for r in world:
+            if r == src or (r in cores and r not in senders) or bays.get(r, 0) >= (BAYS if r in senders else 1):
+                continue
+            if topo.may_write(src, r) and topo.may_write(r, dst):
+                yield r, ways(src, r), ways(r, dst)
+
+    blocks, held = [], {}
+    for p, row in enumerate(dest):
+        for c, q in enumerate(row):
+            src, dst = cores[p], cores[q]
+            blocks.append({"p": p, "c": c, "src": src, "dst": dst, "slot": held.get(q, 0),
+                           "len": min(length(a, b) for _, a, b in relays(src, dst, {}))})
+            held[q] = held.get(q, 0) + 1
+    for p in range(len(dest)):
+        mine = sorted([b for b in blocks if b["p"] == p], key=lambda b: (-b["len"], b["c"]))
+        for i, b in enumerate(mine):
+            b["turn"] = i
+    load, bays = {}, {}
+    for b in sorted(blocks, key=lambda b: (b["turn"], b["p"])):
+        best = None
+        for r, w1, w2 in relays(b["src"], b["dst"], bays):
+            links = set(k for w in w1 + w2 for k in w)
+            hop = int(topo.die(b["src"]) != topo.die(r))
+            key = (length(w1, w2), int(r not in senders), max([load.get(k, 0) + 1 for k in links] + [0]),
+                   len([k for w in w1 for k in w if k[0] != "cable"]) + hop,
+                   hop + int(topo.die(r) != topo.die(b["dst"])), r)
+            if best is None or key < best[0]:
+                best = (key, r, links)
+        b["relay"], b["bay"], b["extra"] = best[1], bays.get(best[1], 0), best[0][1]
+        bays[best[1]] = b["bay"] + 1
+        for k in best[2]:
+            load[k] = load.get(k, 0) + 1
+    _MEMO["routes"] = blocks
+    return blocks
+
+
+def rank_program(g, core, T, topo):
+    blocks = _routes(list(T.cores), T.tables["DEST"], topo)
+    sem = T.sem
+    left = [0]
+
+    def cols(i):
+        return slice(i * TK, (i + 1) * TK)
+
+    def engines(src, dst):
+        return bin(topo.mask(src, dst)).count("1")
+
+    def send(dst, out_ap, in_ap, remote_sem):
+        rid, pid = topo.addr(dst, core)
+        g.remote_dma(out_ap=out_ap, in_ap=in_ap, remote_sem=remote_sem, local_sem=sem.sent, pid=pid, routing_id=rid,
+                     dma_engine_mask=topo.mask(core, dst))
+        left[0] += engines(core, dst)
+
+    mine = sorted([b for b in blocks if b["src"] == core], key=lambda b: b["turn"])
+    if mine:
+        g.scalar.dma_start(T.ws[:], T.w[:]).then_inc(sem.wl, 16)
+        for b in mine:
+            g.sync.dma_start(T.xs[:, cols(b["c"])], T.x[:, cols(b["c"])]).then_inc(sem["xl%d" % b["turn"]], 16)
+        g.vector.memset(T.zero[:], 0.0).then_inc(sem.zs, 1)
+        g.vector.wait_ge(sem.zs, 1)
+        g.tensor.wait_ge(sem.wl, 16)
+        for b in mine:
+            i = b["turn"]
+            acc, h = T["ps%d" % i][:, 0:TK], T["h%d" % i]
+            g.tensor.wait_ge(sem["xl%d" % i], 16)
+            g.tensor.matmul(acc, T.ws[:], T.xs[:, cols(b["c"])], True, True).then_inc(sem["mm%d" % i], 1)
+            g.vector.wait_ge(sem["mm%d" % i], 1)
+            g.vector.tensor_tensor(h[:], acc, T.zero[:], AluOpType.max).then_inc(sem["cp%d" % i], 1)
+            g.wait_ge(sem["cp%d" % i], 1)
+            send(b["relay"], T["bay%d" % b["bay"]][:], h[:], sem["in%d" % b["bay"]])
+
+    for b in sorted([b for b in blocks if b["relay"] == core], key=lambda b: b["bay"]):
+        g.wait_ge(sem["in%d" % b["bay"]], engines(b["src"], core))
+        send(b["dst"], T.land[:, cols(b["slot"])], T["bay%d" % b["bay"]][:], sem["at%d" % b["slot"]])
+    if left[0]:
+        g.wait_ge(sem.sent, left[0])
+
+    owned = sorted([b for b in blocks if b["dst"] == core], key=lambda b: (b["extra"], b["turn"], b["p"]))
+    if owned:
+        g.scalar.dma_start(T.ws[:], T.w[:]).then_inc(sem.wl, 16)
+        g.tensor.wait_ge(sem.wl, 16)
+        for i, b in enumerate(owned):
+            s = b["slot"]
+            acc, queue = T["ps%d" % i][:, 0:TK], (g.sync, g.scalar)[i % 2]
+            g.tensor.wait_ge(sem["at%d" % s], engines(b["relay"], core))
+            g.tensor.matmul(acc, T.ws[:], T.land[:, cols(s)], True, True).then_inc(sem["mm%d" % i], 1)
+            g.vector.wait_ge(sem["mm%d" % i], 1)
+            g.vector.tensor_copy(T.res[:, cols(s)], acc).then_inc(sem["cp%d" % i], 1)
+            queue.wait_ge(sem["cp%d" % i], 1)
+            queue.dma_start(T.y[:, cols(s)], T.res[:, cols(s)]).then_inc(sem["st%d" % i], 16)
+        for i in range(len(owned)):
+            (g.sync, g.scalar)[i % 2].wait_ge(sem["st%d" % i], 16)

@@ -1,6 +1,7 @@
+from concourse.bass import DstId, RemoteDMATransfer
 from concourse.mybir import AluOpType
 
-TK, SLOTS, BAYS = 256, 5, 2
+TK, SLOTS = 256, 5
 
 SCRATCH = {
     "xs": ("sbuf", [128, 2 * TK], "bfloat16"),
@@ -8,15 +9,14 @@ SCRATCH = {
     "zero": ("sbuf", [128, TK], "float32"),
     "h0": ("sbuf", [128, TK], "bfloat16"),
     "h1": ("sbuf", [128, TK], "bfloat16"),
-    "bay0": ("sbuf", [128, TK], "bfloat16"),
-    "bay1": ("sbuf", [128, TK], "bfloat16"),
+    "bay": ("sbuf", [128, TK], "bfloat16"),
     "land": ("sbuf", [128, SLOTS * TK], "bfloat16"),
     "res": ("sbuf", [128, SLOTS * TK], "bfloat16"),
 }
 for _i in range(SLOTS):
     SCRATCH["ps%d" % _i] = ("psum", [128, 512], "float32")
 
-SEMAPHORES = ["wl", "xl0", "xl1", "zs", "sent", "in0", "in1"] + [
+SEMAPHORES = ["wl", "xl0", "xl1", "zs", "sent", "inb"] + [
     "%s%d" % (n, i) for n in ("at", "mm", "cp", "st") for i in range(SLOTS)]
 
 _MEMO = {}
@@ -62,40 +62,28 @@ def _routes(cores, dest, topo):
             return [first]
         return [first, in_rack(a, twin(b, ha), d) + [cable(a, twin(b, ha))]]
 
-    def length(w1, w2):
-        return sum(max(len([k for k in w if k[0] != "in"]) for w in ww) + len(ww) - 1 for ww in (w1, w2))
-
-    def relays(src, dst, bays):
-        for r in world:
-            if r == src or (r in cores and r not in senders) or bays.get(r, 0) >= (BAYS if r in senders else 1):
-                continue
-            if topo.may_write(src, r) and topo.may_write(r, dst):
-                yield r, ways(src, r), ways(r, dst)
-
     blocks, held = [], {}
     for p, row in enumerate(dest):
         for c, q in enumerate(row):
-            src, dst = cores[p], cores[q]
-            blocks.append({"p": p, "c": c, "src": src, "dst": dst, "slot": held.get(q, 0),
-                           "len": min(length(a, b) for _, a, b in relays(src, dst, {}))})
+            blocks.append({"p": p, "c": c, "q": q, "src": cores[p], "dst": cores[q], "slot": held.get(q, 0)})
             held[q] = held.get(q, 0) + 1
-    for p in range(len(dest)):
-        mine = sorted([b for b in blocks if b["p"] == p], key=lambda b: (-b["len"], b["c"]))
-        for i, b in enumerate(mine):
-            b["turn"] = i
-    load, bays = {}, {}
-    for b in sorted(blocks, key=lambda b: (b["turn"], b["p"])):
+    load, taken = {}, set()
+    for b in sorted(blocks, key=lambda b: (-held[b["q"]], b["p"], b["c"])):
         best = None
-        for r, w1, w2 in relays(b["src"], b["dst"], bays):
-            links = set(k for w in w1 + w2 for k in w)
-            hop = int(topo.die(b["src"]) != topo.die(r))
-            key = (length(w1, w2), int(r not in senders), max([load.get(k, 0) + 1 for k in links] + [0]),
-                   len([k for w in w1 for k in w if k[0] != "cable"]) + hop,
-                   hop + int(topo.die(r) != topo.die(b["dst"])), r)
+        for r in world:
+            if r == b["src"] or r in taken or (r in cores and r not in senders):
+                continue
+            if not (topo.may_write(b["src"], r) and topo.may_write(r, b["dst"])):
+                continue
+            w1, w2 = ways(b["src"], r), ways(r, b["dst"])
+            links = set((1, k) for w in w1 for k in w) | set((2, k) for w in w2 for k in w)
+            key = (max([load.get(k, 0) + 1 for k in links] + [0]), len(w1) + len(w2), int(r not in senders),
+                   sum(max(len([k for k in w if k[0] != "in"]) for w in ww) for ww in (w1, w2)),
+                   int(topo.die(b["src"]) != topo.die(r)) + int(topo.die(r) != topo.die(b["dst"])), r)
             if best is None or key < best[0]:
                 best = (key, r, links)
-        b["relay"], b["bay"], b["extra"] = best[1], bays.get(best[1], 0), best[0][1]
-        bays[best[1]] = b["bay"] + 1
+        b["relay"], b["cold"] = best[1], best[0][2]
+        taken.add(best[1])
         for k in best[2]:
             load[k] = load.get(k, 0) + 1
     _MEMO["routes"] = blocks
@@ -110,47 +98,63 @@ def rank_program(g, core, T, topo):
     def cols(i):
         return slice(i * TK, (i + 1) * TK)
 
-    def engines(src, dst):
-        return bin(topo.mask(src, dst)).count("1")
+    def bits(mask):
+        return [1 << i for i in range(mask.bit_length()) if mask >> i & 1]
 
-    def send(dst, out_ap, in_ap, remote_sem):
-        rid, pid = topo.addr(dst, core)
-        g.remote_dma(out_ap=out_ap, in_ap=in_ap, remote_sem=remote_sem, local_sem=sem.sent, pid=pid, routing_id=rid,
-                     dma_engine_mask=topo.mask(core, dst))
-        left[0] += engines(core, dst)
+    def lanes1(b):
+        both = [o for o in blocks if o["src"] == b["src"]]
+        common = topo.mask(b["src"], both[0]["relay"])
+        for o in both:
+            common &= topo.mask(b["src"], o["relay"])
+        return sum(bits(common)[both.index(b)::len(both)])
 
-    mine = sorted([b for b in blocks if b["src"] == core], key=lambda b: b["turn"])
+    def lanes2(b):
+        full = topo.mask(b["relay"], b["dst"])
+        return sum(bits(full)[::2]) if b["cold"] else full
+
+    def count(mask):
+        return len(bits(mask))
+
+    mine = [b for b in blocks if b["src"] == core]
     if mine:
         g.scalar.dma_start(T.ws[:], T.w[:]).then_inc(sem.wl, 16)
-        for b in mine:
-            g.sync.dma_start(T.xs[:, cols(b["c"])], T.x[:, cols(b["c"])]).then_inc(sem["xl%d" % b["turn"]], 16)
+        for i, b in enumerate(mine):
+            g.sync.dma_start(T.xs[:, cols(b["c"])], T.x[:, cols(b["c"])]).then_inc(sem["xl%d" % i], 16)
         g.vector.memset(T.zero[:], 0.0).then_inc(sem.zs, 1)
         g.vector.wait_ge(sem.zs, 1)
         g.tensor.wait_ge(sem.wl, 16)
-        for b in mine:
-            i = b["turn"]
+        out = []
+        for i, b in enumerate(mine):
             acc, h = T["ps%d" % i][:, 0:TK], T["h%d" % i]
             g.tensor.wait_ge(sem["xl%d" % i], 16)
             g.tensor.matmul(acc, T.ws[:], T.xs[:, cols(b["c"])], True, True).then_inc(sem["mm%d" % i], 1)
             g.vector.wait_ge(sem["mm%d" % i], 1)
             g.vector.tensor_tensor(h[:], acc, T.zero[:], AluOpType.max).then_inc(sem["cp%d" % i], 1)
             g.wait_ge(sem["cp%d" % i], 1)
-            send(b["relay"], T["bay%d" % b["bay"]][:], h[:], sem["in%d" % b["bay"]])
+            rid, pid = topo.addr(b["relay"], core)
+            out.append(RemoteDMATransfer(dst_ids=[DstId(rid=rid, pnc=pid)], dma_engine_mask=lanes1(b), remote_sem=sem.inb,
+                                         src=h[:], dst=T.bay[:]))
+            left[0] += count(lanes1(b))
+        g.remote_dma_fused(out, local_sem=sem.sent)
 
-    for b in sorted([b for b in blocks if b["relay"] == core], key=lambda b: b["bay"]):
-        g.wait_ge(sem["in%d" % b["bay"]], engines(b["src"], core))
-        send(b["dst"], T.land[:, cols(b["slot"])], T["bay%d" % b["bay"]][:], sem["at%d" % b["slot"]])
+    for b in blocks:
+        if b["relay"] == core:
+            g.wait_ge(sem.inb, count(lanes1(b)))
+            rid, pid = topo.addr(b["dst"], core)
+            g.remote_dma(out_ap=T.land[:, cols(b["slot"])], in_ap=T.bay[:], remote_sem=sem["at%d" % b["slot"]],
+                         local_sem=sem.sent, pid=pid, routing_id=rid, dma_engine_mask=lanes2(b))
+            left[0] += count(lanes2(b))
     if left[0]:
         g.wait_ge(sem.sent, left[0])
 
-    owned = sorted([b for b in blocks if b["dst"] == core], key=lambda b: (b["extra"], b["turn"], b["p"]))
+    owned = sorted([b for b in blocks if b["dst"] == core], key=lambda b: (b["cold"], b["p"], b["c"]))
     if owned:
         g.scalar.dma_start(T.ws[:], T.w[:]).then_inc(sem.wl, 16)
         g.tensor.wait_ge(sem.wl, 16)
         for i, b in enumerate(owned):
             s = b["slot"]
             acc, queue = T["ps%d" % i][:, 0:TK], (g.sync, g.scalar)[i % 2]
-            g.tensor.wait_ge(sem["at%d" % s], engines(b["relay"], core))
+            g.tensor.wait_ge(sem["at%d" % s], count(lanes2(b)))
             g.tensor.matmul(acc, T.ws[:], T.land[:, cols(s)], True, True).then_inc(sem["mm%d" % i], 1)
             g.vector.wait_ge(sem["mm%d" % i], 1)
             g.vector.tensor_copy(T.res[:, cols(s)], acc).then_inc(sem["cp%d" % i], 1)

@@ -1,23 +1,25 @@
 from concourse.bass import DstId, RemoteDMATransfer
 from concourse.mybir import AluOpType
 
-TK, SLOTS = 256, 5
+TK, SLOTS, HALVES, BANKS = 256, 5, 2, 8
+HK = TK // HALVES
+NPC = SLOTS * HALVES
 
 SCRATCH = {
     "xs": ("sbuf", [128, 2 * TK], "bfloat16"),
     "ws": ("sbuf", [128, 128], "bfloat16"),
-    "zero": ("sbuf", [128, TK], "float32"),
+    "zero": ("sbuf", [128, HK], "float32"),
     "h0": ("sbuf", [128, TK], "bfloat16"),
     "h1": ("sbuf", [128, TK], "bfloat16"),
     "bay": ("sbuf", [128, TK], "bfloat16"),
     "land": ("sbuf", [128, SLOTS * TK], "bfloat16"),
     "res": ("sbuf", [128, SLOTS * TK], "bfloat16"),
 }
-for _i in range(SLOTS):
+for _i in range(BANKS):
     SCRATCH["ps%d" % _i] = ("psum", [128, 512], "float32")
 
-SEMAPHORES = ["wl", "xl0", "xl1", "zs", "sent", "inb"] + [
-    "%s%d" % (n, i) for n in ("at", "mm", "cp", "st") for i in range(SLOTS)]
+SEMAPHORES = ["wl", "xl", "zs", "sent"] + ["in%d" % j for j in range(HALVES)] + [
+    "%s%d" % (n, i) for n in ("at", "mm", "cp", "st") for i in range(NPC)]
 
 _MEMO = {}
 
@@ -62,30 +64,61 @@ def _routes(cores, dest, topo):
             return [first]
         return [first, in_rack(a, twin(b, ha), d) + [cable(a, twin(b, ha))]]
 
+    def turns(b, r):
+        return int(topo.die(b["src"]) != topo.die(r)) + int(topo.die(r) != topo.die(b["dst"]))
+
     blocks, held = [], {}
     for p, row in enumerate(dest):
         for c, q in enumerate(row):
             blocks.append({"p": p, "c": c, "q": q, "src": cores[p], "dst": cores[q], "slot": held.get(q, 0)})
             held[q] = held.get(q, 0) + 1
+    order = sorted(blocks, key=lambda b: (-held[b["q"]], b["p"], b["c"]))
     load, taken = {}, set()
-    for b in sorted(blocks, key=lambda b: (-held[b["q"]], b["p"], b["c"])):
+
+    def open_to(b, r):
+        return (r != b["src"] and r not in taken and (r not in cores or r in senders)
+                and topo.may_write(b["src"], r) and topo.may_write(r, b["dst"]))
+
+    for b in order:
         best = None
         for r in world:
-            if r == b["src"] or r in taken or (r in cores and r not in senders):
-                continue
-            if not (topo.may_write(b["src"], r) and topo.may_write(r, b["dst"])):
+            if not open_to(b, r):
                 continue
             w1, w2 = ways(b["src"], r), ways(r, b["dst"])
             links = set((1, k) for w in w1 for k in w) | set((2, k) for w in w2 for k in w)
             key = (max([load.get(k, 0) + 1 for k in links] + [0]), len(w1) + len(w2), int(r not in senders),
-                   sum(max(len([k for k in w if k[0] != "in"]) for w in ww) for ww in (w1, w2)),
-                   int(topo.die(b["src"]) != topo.die(r)) + int(topo.die(r) != topo.die(b["dst"])), r)
+                   sum(max(len([k for k in w if k[0] != "in"]) for w in ww) for ww in (w1, w2)), turns(b, r), r)
             if best is None or key < best[0]:
                 best = (key, r, links)
-        b["relay"], b["cold"] = best[1], best[0][2]
+        b["relays"], b["links"] = [best[1]] * HALVES, best[2]
         taken.add(best[1])
         for k in best[2]:
             load[k] = load.get(k, 0) + 1
+    over = {}
+    for b in order:
+        for n, k in b["links"]:
+            if n == 1 and k[0] == "cable":
+                over[k] = over.get(k, 0) + HALVES
+    for b in order:
+        if [k for n, k in b["links"] if n == 2 and k[0] == "cable"]:
+            at = b["relays"][0]
+            taken.discard(at)
+            for j in range(HALVES):
+                best = None
+                for r in world:
+                    if place(r) != place(at) or not open_to(b, r):
+                        continue
+                    mine = set(k for w in ways(r, b["dst"]) for k in w if k[0] == "cable")
+                    key = (max(over.get(k, 0) + 1 for k in mine), sum(over.get(k, 0) + 1 for k in mine),
+                           int(r not in senders), turns(b, r), r)
+                    if best is None or key < best[0]:
+                        best = (key, r, mine)
+                b["relays"][j] = best[1]
+                taken.add(best[1])
+                for k in best[2]:
+                    over[k] = over.get(k, 0) + 1
+    for b in blocks:
+        b["cold"] = [int(r not in senders) for r in b["relays"]]
     _MEMO["routes"] = blocks
     return blocks
 
@@ -95,22 +128,22 @@ def rank_program(g, core, T, topo):
     sem = T.sem
     left = [0]
 
-    def cols(i):
-        return slice(i * TK, (i + 1) * TK)
+    def half(base, j):
+        return slice(base * TK + j * HK, base * TK + (j + 1) * HK)
 
     def bits(mask):
         return [1 << i for i in range(mask.bit_length()) if mask >> i & 1]
 
-    def lanes1(b):
+    def lanes1(b, j):
         both = [o for o in blocks if o["src"] == b["src"]]
-        common = topo.mask(b["src"], both[0]["relay"])
+        common = topo.mask(b["src"], b["relays"][j])
         for o in both:
-            common &= topo.mask(b["src"], o["relay"])
+            common &= topo.mask(b["src"], o["relays"][j])
         return sum(bits(common)[both.index(b)::len(both)])
 
-    def lanes2(b):
-        full = topo.mask(b["relay"], b["dst"])
-        return sum(bits(full)[::2]) if b["cold"] else full
+    def lanes2(b, j):
+        full = topo.mask(b["relays"][j], b["dst"])
+        return sum(bits(full)[::2]) if b["cold"][j] else full
 
     def count(mask):
         return len(bits(mask))
@@ -118,47 +151,52 @@ def rank_program(g, core, T, topo):
     mine = [b for b in blocks if b["src"] == core]
     if mine:
         g.scalar.dma_start(T.ws[:], T.w[:]).then_inc(sem.wl, 16)
-        for i, b in enumerate(mine):
-            g.sync.dma_start(T.xs[:, cols(b["c"])], T.x[:, cols(b["c"])]).then_inc(sem["xl%d" % i], 16)
+        g.sync.dma_start(T.xs[:], T.x[:]).then_inc(sem.xl, 16)
         g.vector.memset(T.zero[:], 0.0).then_inc(sem.zs, 1)
         g.vector.wait_ge(sem.zs, 1)
         g.tensor.wait_ge(sem.wl, 16)
-        out = []
-        for i, b in enumerate(mine):
-            acc, h = T["ps%d" % i][:, 0:TK], T["h%d" % i]
-            g.tensor.wait_ge(sem["xl%d" % i], 16)
-            g.tensor.matmul(acc, T.ws[:], T.xs[:, cols(b["c"])], True, True).then_inc(sem["mm%d" % i], 1)
-            g.vector.wait_ge(sem["mm%d" % i], 1)
-            g.vector.tensor_tensor(h[:], acc, T.zero[:], AluOpType.max).then_inc(sem["cp%d" % i], 1)
-            g.wait_ge(sem["cp%d" % i], 1)
-            rid, pid = topo.addr(b["relay"], core)
-            out.append(RemoteDMATransfer(dst_ids=[DstId(rid=rid, pnc=pid)], dma_engine_mask=lanes1(b), remote_sem=sem.inb,
-                                         src=h[:], dst=T.bay[:]))
-            left[0] += count(lanes1(b))
-        g.remote_dma_fused(out, local_sem=sem.sent)
+        g.tensor.wait_ge(sem.xl, 16)
+        for j in range(HALVES):
+            out = []
+            for i, b in enumerate(mine):
+                n = j * len(mine) + i
+                acc, h = T["ps%d" % n][:, 0:HK], T["h%d" % i][:, half(0, j)]
+                g.tensor.matmul(acc, T.ws[:], T.xs[:, half(b["c"], j)], True, True).then_inc(sem["mm%d" % n], 1)
+                g.vector.wait_ge(sem["mm%d" % n], 1)
+                g.vector.tensor_tensor(h, acc, T.zero[:], AluOpType.max).then_inc(sem["cp%d" % n], 1)
+                g.wait_ge(sem["cp%d" % n], 1)
+                rid, pid = topo.addr(b["relays"][j], core)
+                out.append(RemoteDMATransfer(dst_ids=[DstId(rid=rid, pnc=pid)], dma_engine_mask=lanes1(b, j),
+                                             remote_sem=sem["in%d" % j], src=h, dst=T.bay[:, half(0, j)]))
+                left[0] += count(lanes1(b, j))
+            g.remote_dma_fused(out, local_sem=sem.sent)
 
-    for b in blocks:
-        if b["relay"] == core:
-            g.wait_ge(sem.inb, count(lanes1(b)))
-            rid, pid = topo.addr(b["dst"], core)
-            g.remote_dma(out_ap=T.land[:, cols(b["slot"])], in_ap=T.bay[:], remote_sem=sem["at%d" % b["slot"]],
-                         local_sem=sem.sent, pid=pid, routing_id=rid, dma_engine_mask=lanes2(b))
-            left[0] += count(lanes2(b))
+    for j in range(HALVES):
+        for b in blocks:
+            if b["relays"][j] == core:
+                g.wait_ge(sem["in%d" % j], count(lanes1(b, j)))
+                rid, pid = topo.addr(b["dst"], core)
+                g.remote_dma(out_ap=T.land[:, half(b["slot"], j)], in_ap=T.bay[:, half(0, j)],
+                             remote_sem=sem["at%d" % (b["slot"] * HALVES + j)], local_sem=sem.sent, pid=pid, routing_id=rid,
+                             dma_engine_mask=lanes2(b, j))
+                left[0] += count(lanes2(b, j))
     if left[0]:
         g.wait_ge(sem.sent, left[0])
 
-    owned = sorted([b for b in blocks if b["dst"] == core], key=lambda b: (b["cold"], b["p"], b["c"]))
+    owned = sorted([(b["cold"][j], j, b["p"], b["c"], b["slot"], lanes2(b, j)) for b in blocks if b["dst"] == core
+                    for j in range(HALVES)])
     if owned:
         g.scalar.dma_start(T.ws[:], T.w[:]).then_inc(sem.wl, 16)
         g.tensor.wait_ge(sem.wl, 16)
-        for i, b in enumerate(owned):
-            s = b["slot"]
-            acc, queue = T["ps%d" % i][:, 0:TK], (g.sync, g.scalar)[i % 2]
-            g.tensor.wait_ge(sem["at%d" % s], count(lanes2(b)))
-            g.tensor.matmul(acc, T.ws[:], T.land[:, cols(s)], True, True).then_inc(sem["mm%d" % i], 1)
+        for i, (_, j, _, _, s, lanes) in enumerate(owned):
+            acc, queue = T["ps%d" % (i % BANKS)][:, 0:HK], (g.sync, g.scalar)[i % 2]
+            g.tensor.wait_ge(sem["at%d" % (s * HALVES + j)], count(lanes))
+            if i >= BANKS:
+                g.tensor.wait_ge(sem["cp%d" % (i - BANKS)], 1)
+            g.tensor.matmul(acc, T.ws[:], T.land[:, half(s, j)], True, True).then_inc(sem["mm%d" % i], 1)
             g.vector.wait_ge(sem["mm%d" % i], 1)
-            g.vector.tensor_copy(T.res[:, cols(s)], acc).then_inc(sem["cp%d" % i], 1)
+            g.vector.tensor_copy(T.res[:, half(s, j)], acc).then_inc(sem["cp%d" % i], 1)
             queue.wait_ge(sem["cp%d" % i], 1)
-            queue.dma_start(T.y[:, cols(s)], T.res[:, cols(s)]).then_inc(sem["st%d" % i], 16)
+            queue.dma_start(T.y[:, half(s, j)], T.res[:, half(s, j)]).then_inc(sem["st%d" % i], 16)
         for i in range(len(owned)):
             (g.sync, g.scalar)[i % 2].wait_ge(sem["st%d" % i], 16)

from concourse.bass import DstId, RemoteDMATransfer
from concourse.mybir import AluOpType

TK, SLOTS, HALVES, BANKS = 256, 5, 2, 8
HK = TK // HALVES
NPC = SLOTS * HALVES

SCRATCH = {
    "xs": ("sbuf", [128, 2 * TK], "bfloat16"),
    "ws": ("sbuf", [128, 128], "bfloat16"),
    "zero": ("sbuf", [128, HK], "float32"),
    "h0": ("sbuf", [128, TK], "bfloat16"),
    "h1": ("sbuf", [128, TK], "bfloat16"),
    "bay": ("sbuf", [128, TK], "bfloat16"),
    "land": ("sbuf", [128, SLOTS * TK], "bfloat16"),
    "res": ("sbuf", [128, SLOTS * TK], "bfloat16"),
}
for _i in range(BANKS):
    SCRATCH["ps%d" % _i] = ("psum", [128, 512], "float32")

SEMAPHORES = ["wl", "xl", "zs", "sent"] + ["in%d" % j for j in range(HALVES)] + [
    "%s%d" % (n, i) for n in ("at", "mm", "cp", "st") for i in range(NPC)]

_MEMO = {}


def _routes(cores, dest, topo):
    if "routes" in _MEMO:
        return _MEMO["routes"]
    per_host = topo.CORES_PER_HOST
    world = range(per_host * (1 + max(topo.host(c) for c in cores)))
    senders = cores[:len(dest)]
    mate_memo = {}

    def place(c):
        return (topo.host(c), topo.chip(c))

    def mate_core(c):
        if place(c) not in mate_memo:
            mate_memo[place(c)] = [m for m in world if topo.mates(c, m)][0]
        return mate_memo[place(c)]

    def twin(c, h):
        return c % per_host + h * per_host

    def cable(c, at):
        return ("cable", place(at), topo.die(c), topo.may_write(c, mate_core(c)))

    def in_rack(a, b, d):
        if place(a) == place(b):
            return []
        if topo.mates(a, b):
            return [("mate", place(a), d)]
        if topo.same_plane(a, b):
            return [("out", place(a), d), ("in", place(b), d)]
        return [("mate", place(a), d)] + in_rack(mate_core(a), b, d)

    def ways(a, b):
        d, ha, hb = topo.die(a), topo.host(a), topo.host(b)
        if topo.rack(ha) == topo.rack(hb):
            return [in_rack(a, b, d)]
        first = [cable(a, a)] + in_rack(twin(a, hb), b, d)
        if topo.chip(a) == topo.chip(b):
            return [first]
        return [first, in_rack(a, twin(b, ha), d) + [cable(a, twin(b, ha))]]

    def turns(b, r):
        return int(topo.die(b["src"]) != topo.die(r)) + int(topo.die(r) != topo.die(b["dst"]))

    blocks, held = [], {}
    for p, row in enumerate(dest):
        for c, q in enumerate(row):
            blocks.append({"p": p, "c": c, "q": q, "src": cores[p], "dst": cores[q], "slot": held.get(q, 0)})
            held[q] = held.get(q, 0) + 1
    order = sorted(blocks, key=lambda b: (-held[b["q"]], b["p"], b["c"]))
    load, taken = {}, set()

    def open_to(b, r):
        return (r != b["src"] and r not in taken and (r not in cores or r in senders)
                and topo.may_write(b["src"], r) and topo.may_write(r, b["dst"]))

    for b in order:
        best = None
        for r in world:
            if not open_to(b, r):
                continue
            w1, w2 = ways(b["src"], r), ways(r, b["dst"])
            links = set((1, k) for w in w1 for k in w) | set((2, k) for w in w2 for k in w)
            key = (max([load.get(k, 0) + 1 for k in links] + [0]), len(w1) + len(w2), int(r not in senders),
                   sum(max(len([k for k in w if k[0] != "in"]) for w in ww) for ww in (w1, w2)), turns(b, r), r)
            if best is None or key < best[0]:
                best = (key, r, links)
        b["relays"], b["links"] = [best[1]] * HALVES, best[2]
        taken.add(best[1])
        for k in best[2]:
            load[k] = load.get(k, 0) + 1
    over = {}
    for b in order:
        for n, k in b["links"]:
            if n == 1 and k[0] == "cable":
                over[k] = over.get(k, 0) + HALVES
    for b in order:
        if [k for n, k in b["links"] if n == 2 and k[0] == "cable"]:
            at = b["relays"][0]
            taken.discard(at)
            for j in range(HALVES):
                best = None
                for r in world:
                    if place(r) != place(at) or not open_to(b, r):
                        continue
                    mine = set(k for w in ways(r, b["dst"]) for k in w if k[0] == "cable")
                    key = (max(over.get(k, 0) + 1 for k in mine), sum(over.get(k, 0) + 1 for k in mine),
                           int(r not in senders), turns(b, r), r)
                    if best is None or key < best[0]:
                        best = (key, r, mine)
                b["relays"][j] = best[1]
                taken.add(best[1])
                for k in best[2]:
                    over[k] = over.get(k, 0) + 1
    for b in blocks:
        b["cold"] = [int(r not in senders) for r in b["relays"]]
    _MEMO["routes"] = blocks
    return blocks


def rank_program(g, core, T, topo):
    blocks = _routes(list(T.cores), T.tables["DEST"], topo)
    sem = T.sem
    left = [0]

    def half(base, j):
        return slice(base * TK + j * HK, base * TK + (j + 1) * HK)

    def bits(mask):
        return [1 << i for i in range(mask.bit_length()) if mask >> i & 1]

    def lanes1(b, j):
        both = [o for o in blocks if o["src"] == b["src"]]
        common = topo.mask(b["src"], b["relays"][j])
        for o in both:
            common &= topo.mask(b["src"], o["relays"][j])
        return sum(bits(common)[both.index(b)::len(both)])

    def lanes2(b, j):
        full = topo.mask(b["relays"][j], b["dst"])
        return sum(bits(full)[::2]) if b["cold"][j] else full

    def count(mask):
        return len(bits(mask))

    mine = [b for b in blocks if b["src"] == core]
    if mine:
        g.scalar.dma_start(T.ws[:], T.w[:]).then_inc(sem.wl, 16)
        g.sync.dma_start(T.xs[:], T.x[:]).then_inc(sem.xl, 16)
        g.vector.memset(T.zero[:], 0.0).then_inc(sem.zs, 1)
        g.vector.wait_ge(sem.zs, 1)
        g.tensor.wait_ge(sem.wl, 16)
        g.tensor.wait_ge(sem.xl, 16)
        for j in range(HALVES):
            out = []
            for i, b in enumerate(mine):
                n = j * len(mine) + i
                acc, h = T["ps%d" % n][:, 0:HK], T["h%d" % i][:, half(0, j)]
                g.tensor.matmul(acc, T.ws[:], T.xs[:, half(b["c"], j)], True, True).then_inc(sem["mm%d" % n], 1)
                g.vector.wait_ge(sem["mm%d" % n], 1)
                g.vector.tensor_tensor(h, acc, T.zero[:], AluOpType.max).then_inc(sem["cp%d" % n], 1)
                g.wait_ge(sem["cp%d" % n], 1)
                rid, pid = topo.addr(b["relays"][j], core)
                out.append(RemoteDMATransfer(dst_ids=[DstId(rid=rid, pnc=pid)], dma_engine_mask=lanes1(b, j),
                                             remote_sem=sem["in%d" % j], src=h, dst=T.bay[:, half(0, j)]))
                left[0] += count(lanes1(b, j))
            g.remote_dma_fused(out, local_sem=sem.sent)

    for j in range(HALVES):
        for b in blocks:
            if b["relays"][j] == core:
                g.wait_ge(sem["in%d" % j], count(lanes1(b, j)))
                rid, pid = topo.addr(b["dst"], core)
                g.remote_dma(out_ap=T.land[:, half(b["slot"], j)], in_ap=T.bay[:, half(0, j)],
                             remote_sem=sem["at%d" % (b["slot"] * HALVES + j)], local_sem=sem.sent, pid=pid, routing_id=rid,
                             dma_engine_mask=lanes2(b, j))
                left[0] += count(lanes2(b, j))
    if left[0]:
        g.wait_ge(sem.sent, left[0])

    owned = sorted([(b["cold"][j], j, b["p"], b["c"], b["slot"], lanes2(b, j)) for b in blocks if b["dst"] == core
                    for j in range(HALVES)])
    if owned:
        g.scalar.dma_start(T.ws[:], T.w[:]).then_inc(sem.wl, 16)
        g.tensor.wait_ge(sem.wl, 16)
        for i, (_, j, _, _, s, lanes) in enumerate(owned):
            acc, queue = T["ps%d" % (i % BANKS)][:, 0:HK], (g.sync, g.scalar)[i % 2]
            g.tensor.wait_ge(sem["at%d" % (s * HALVES + j)], count(lanes))
            if i >= BANKS:
                g.tensor.wait_ge(sem["cp%d" % (i - BANKS)], 1)
            g.tensor.matmul(acc, T.ws[:], T.land[:, half(s, j)], True, True).then_inc(sem["mm%d" % i], 1)
            g.vector.wait_ge(sem["mm%d" % i], 1)
            g.vector.tensor_copy(T.res[:, half(s, j)], acc).then_inc(sem["cp%d" % i], 1)
            queue.wait_ge(sem["cp%d" % i], 1)
            queue.dma_start(T.y[:, half(s, j)], T.res[:, half(s, j)]).then_inc(sem["st%d" % i], 16)
        for i in range(len(owned)):
            (g.sync, g.scalar)[i % 2].wait_ge(sem["st%d" % i], 16)
